import numpy as np
import ml_dtypes


def mxq(x, axis, fmt="e4m3"):
    dtype, down = {"e4m3": (ml_dtypes.float8_e4m3fn, 7), "e5m2": (ml_dtypes.float8_e5m2, 14)}[fmt]
    v = np.moveaxis(np.asarray(x, np.float32).astype(ml_dtypes.bfloat16).astype(np.float64), axis, -1)
    blocks = v.reshape(v.shape[:-1] + (-1, 32))
    amax = np.abs(blocks).max(-1, keepdims=True)
    byte = np.maximum(np.where(amax > 0, np.frexp(amax)[1] - 1 + 127, 0) - down, 1)
    scale = np.exp2(byte - 127.0)
    codes = (blocks / scale).astype(np.float32).astype(dtype).astype(np.float64)
    return np.moveaxis((codes * scale).reshape(v.shape), -1, axis)


WIDE = False


def mx_kscale(k):
    if not WIDE:
        return np.ones(k)
    levels = np.array([30, -30])
    if k % 512:
        return np.exp2(np.random.permutation(np.resize(levels, k // 32))).repeat(32)
    a = np.empty((k // 512, 16))
    for p in range(k // 512):
        a[p, :8] = np.random.permutation(np.resize(levels, 8))
        for g in range(8):
            far = levels[np.abs(levels - a[p, g]) >= 10]
            a[p, g + 8] = far[np.random.randint(len(far))]
    return np.exp2(a.ravel()).repeat(32)


def f64(x):
    return np.asarray(x).astype(np.float64)


def striped(idx):
    return np.tile(np.asarray(idx).reshape(-1, 16).T, (8, 1)).astype(np.uint16)


def unstriped(offs):
    return offs[:16].T.reshape(-1).astype(np.int64)


E2M1 = np.array([0.0, 0.5, 1.0, 1.5, 2.0, 3.0, 4.0, 6.0, -0.0, -0.5, -1.0, -1.5, -2.0, -3.0, -4.0, -6.0])


def pack_weight(w, fmt):
    k, n = w.shape
    w = f64(np.asarray(w, np.float32).astype(ml_dtypes.bfloat16)).reshape(k // 32, 32, n)
    amax = np.abs(w).max(1)
    if fmt in ("e4m3", "e5m2"):
        byte = np.frexp(amax)[1] - 1 + 127 - (7 if fmt == "e4m3" else 14)
    else:
        mant, ex = np.frexp(amax / 6.0)
        byte = np.where(mant > 0.5, ex, ex - 1) + 127
    byte = np.clip(np.where(amax > 0, byte, 1), 1, 254)
    scaled = (w * np.exp2(127.0 - byte)[:, None, :]).reshape(k, n).astype(np.float32)
    by_word = np.ascontiguousarray(scaled.reshape(k // 512, 128, 4, n).transpose(0, 1, 3, 2))
    if fmt in ("e4m3", "e5m2"):
        words = by_word.astype(ml_dtypes.float8_e4m3fn if fmt == "e4m3" else ml_dtypes.float8_e5m2).view(np.uint8)
    else:
        c = by_word.astype(ml_dtypes.float4_e2m1fn).view(np.uint8) & 0xF
        words = (c[..., 0::2] | (c[..., 1::2] << 4)).reshape(k // 512, 128, 2 * n)
    return np.ascontiguousarray(words), np.ascontiguousarray(byte.astype(np.uint8).reshape(k // 512, 16, n))


def unpack_weight(words, scales, fmt):
    g, _, n = scales.shape
    words = np.ascontiguousarray(words).reshape(g, 128, n, -1)
    if fmt in ("e4m3", "e5m2"):
        vals = words.view(ml_dtypes.float8_e4m3fn if fmt == "e4m3" else ml_dtypes.float8_e5m2).astype(np.float64)
    else:
        nib = np.empty((g, 128, n, 4), np.uint8)
        nib[..., 0::2] = words & 0xF
        nib[..., 1::2] = words >> 4
        vals = E2M1[nib]
    vals = vals * np.repeat(np.exp2(scales.astype(np.float64) - 127.0), 8, axis=1)[..., None]
    return vals.transpose(0, 1, 3, 2).reshape(g * 512, n)


K, T, J, B, R, V, N = 1024, 1024, 384, 48, 512, 512, 256


def setup_inputs():
    n = np.random.standard_normal
    idx = np.random.permutation(T)[:J]
    idx2 = np.random.permutation(V)[:J]
    fk = mx_kscale(K)
    fr = mx_kscale(R)
    wp = pack_weight(n((K, R)) * 1 / np.sqrt(K) * fk[:, None] * fr, "e2m1")
    wbp = pack_weight(n((R, N)) * 1 / np.sqrt(R) / fr[:, None], "e5m2")
    return {
        "xf": (n((K, T))).astype(np.float32),
        "fk": (np.random.uniform(0.5, 2.0, (K, 1)) / fk[:, None]).astype(np.float32),
        "w_words": wp[0],
        "w_scales": wp[1],
        "tb": (n((R, V)) * 0.7 * fr[:, None]).astype(np.float32),
        "wb_words": wbp[0],
        "wb_scales": wbp[1],
        "rs": (n((N, J))).astype(np.float32),
        "offs": striped(idx),
        "offs2": striped(idx2),
    }


def reference(xf, fk, w_words, w_scales, tb, wb_words, wb_scales, rs, offs, offs2):
    idx = unstriped(offs)
    idx2 = unstriped(offs2)
    wu = unpack_weight(w_words, w_scales, "e2m1")
    wbu = unpack_weight(wb_words, wb_scales, "e5m2")
    xg = f64(xf)[:, idx]
    g1 = xg.reshape(K, B, J // B).mean(axis=2)
    g2 = np.repeat(g1, J // B, axis=1)
    u = (xg - g2) * f64(fk)
    uq = mxq(u, 0, "e4m3")
    a = wu.T @ uq
    hid = np.maximum(a - f64(tb)[:, idx2], 0.0)
    hidq = mxq(hid, 0, "e4m3")
    p = wbu.T @ hidq
    p1 = np.pad(p, ((0, 0), (1, 0)))[:, :J]
    y = p - 0.7 * p1 + 0.5 * f64(rs)
    return y

@@ -1,0 +1,266 @@
+from contextlib import ExitStack
+
+import concourse.mybir as mybir
+
+K, T, J, R, V, N = 1024, 1024, 384, 512, 512, 256
+GROUP = 8
+B = J // GROUP
+FLOPS = 2 * K * R * J + 2 * R * N * J
+
+F32 = mybir.dt.float32
+BF16 = mybir.dt.bfloat16
+I32 = mybir.dt.int32
+U32 = mybir.dt.uint32
+U16 = mybir.dt.uint16
+U8 = mybir.dt.uint8
+E4M3X4 = mybir.dt.float8_e4m3fn_x4
+E5M2X4 = mybir.dt.float8_e5m2_x4
+E2M1X4 = mybir.dt.float4_e2m1fn_x4
+ALU = mybir.AluOpType
+ACT = mybir.ActivationFunctionType
+
+P = 128
+PACK = 4
+PASSES = K // (P * PACK)
+CHUNK = 128
+CHUNKS = J // CHUNK
+HALVES = N // P
+LIST_COLS = J // 16
+RUN = 4
+
+
+def tile_list_centredpicks_overtable_lagged_kernel(
+    tc, xf, fk, w_words, w_scales, tb, wb_words, wb_scales, rs, offs, offs2, out
+):
+    nc = tc.nc
+    with ExitStack() as ctx:
+        pool = ctx.enter_context(tc.tile_pool(name="held", bufs=1))
+        psum = ctx.enter_context(tc.psum_pool(name="psum", bufs=1))
+
+        def tile(shape, dtype, name):
+            return pool.tile(shape, dtype, name=name, align_bytes=64)
+
+        planes = [(a, t) for a in range(PASSES) for t in range(PACK)]
+        x_list = tile([P, LIST_COLS], U16, "x_list")
+        tb_list = tile([P, LIST_COLS], U16, "tb_list")
+        x_rows = {(a, t): tile([P, T], F32, "x_rows%d%d" % (a, t)) for a, t in planes}
+        x_picked = {(a, t): tile([P, J], F32, "x_picked%d%d" % (a, t)) for a, t in planes}
+        sums = {(a, t): tile([P, B], F32, "sums%d%d" % (a, t)) for a, t in planes}
+        means = {(a, t): tile([P, B], F32, "means%d%d" % (a, t)) for a, t in planes}
+        fk_sb = tile([P, PASSES, PACK], F32, "fk_sb")
+        fk_eighth = tile([P, PASSES, PACK], F32, "fk_eighth")
+        u_planes = [tile([P, PACK, J], BF16, "u_planes%d" % a) for a in range(PASSES)]
+        u_woven = [tile([P, J * PACK], BF16, "u_woven%d" % a) for a in range(PASSES)]
+        u_codes = [tile([P, J], U32, "u_codes%d" % a) for a in range(PASSES)]
+        u_scales = [tile([P, J], U8, "u_scales%d" % a) for a in range(PASSES)]
+        w_raw = tile([P, PASSES, R], U16, "w_raw")
+        w_dealt = tile([P, PASSES, PACK, P], U16, "w_dealt")
+        ws_raw = tile([P, PASSES, R], U8, "ws_raw")
+        ws_dealt = tile([P, PASSES, PACK, P], U8, "ws_dealt")
+        tb_rows = [tile([P, V], F32, "tb_rows%d" % t) for t in range(PACK)]
+        tb_picked = tile([P, PACK, J], F32, "tb_picked")
+        wb_codes = tile([P, N], U32, "wb_codes")
+        wb_plane = tile([P, N], U8, "wb_plane")
+        lagged = tile([P, HALVES, J], F32, "lagged")
+        result = tile([P, HALVES, J], F32, "result")
+        gaps = [tile([P, PACK, CHUNK], F32, "gaps%d" % c) for c in range(CHUNKS)]
+        hid_woven = [tile([P, CHUNK * PACK], BF16, "hid_woven%d" % c) for c in range(CHUNKS)]
+        hid_codes = [tile([P, CHUNK], U32, "hid_codes%d" % c) for c in range(CHUNKS)]
+        hid_scales = [tile([P, CHUNK], U8, "hid_scales%d" % c) for c in range(CHUNKS)]
+        a_banks = [psum.tile([P, PACK, CHUNK], F32, name="a_bank%d" % c) for c in range(CHUNKS)]
+        p_banks = [psum.tile([P, HALVES, CHUNK], F32, name="p_bank%d" % c) for c in range(CHUNKS)]
+
+        x_hbm = xf.rearrange("(a p t) c -> a t p c", a=PASSES, t=PACK)
+        tb_hbm = tb.rearrange("(p t) v -> t p v", t=PACK)
+
+        nc.gpsimd.memset(ws_raw[:].bitcast(I32), 0)
+        nc.gpsimd.memset(wb_plane[:].bitcast(I32), 0)
+        nc.sync.dma_start(x_list[:], offs)
+        nc.sync.dma_start(out=x_rows[0, 0][:], in_=x_hbm[0, 0])
+        nc.sync.dma_start(out=fk_sb[:], in_=fk.rearrange("(a p t) o -> p a (t o)", a=PASSES, t=PACK))
+        nc.sync.dma_start(
+            out=w_raw[:].bitcast(I32), in_=w_words.rearrange("a p c -> p a c").bitcast(I32)
+        )
+        for a, t in planes[1:5]:
+            nc.sync.dma_start(out=x_rows[a, t][:], in_=x_hbm[a, t])
+        for q in range(4):
+            nc.sync.dma_start(
+                out=ws_raw[32 * q : 32 * q + 4].bitcast(I32),
+                in_=w_scales[:, 4 * q : 4 * q + 4, :].rearrange("a r c -> r a c").bitcast(I32),
+            )
+        for a, t in planes[5:]:
+            nc.sync.dma_start(out=x_rows[a, t][:], in_=x_hbm[a, t])
+        nc.sync.dma_start(tb_list[:], offs2)
+        for t in range(PACK):
+            nc.sync.dma_start(out=tb_rows[t][:], in_=tb_hbm[t])
+        nc.sync.dma_start(
+            out=wb_codes[:].bitcast(I32), in_=wb_words[0].rearrange("p n t -> p (n t)").bitcast(I32)
+        )
+        for q in range(4):
+            nc.sync.dma_start(
+                out=wb_plane[32 * q : 32 * q + 4].bitcast(I32),
+                in_=wb_scales[0, 4 * q : 4 * q + 4, :].bitcast(I32),
+            )
+        nc.sync.dma_start(out=lagged[:], in_=rs.rearrange("(h p) j -> p h j", p=P))
+
+        nc.scalar.activation(out=fk_eighth[:], in_=fk_sb[:], func=ACT.Copy, scale=1.0 / GROUP)
+        nc.vector.tensor_copy(out=w_dealt[:], in_=w_raw[:].rearrange("p a (m t) -> p a t m", t=PACK))
+        nc.vector.tensor_copy(out=ws_dealt[:], in_=ws_raw[:].rearrange("p a (m t) -> p a t m", t=PACK))
+
+        def slots(c):
+            return slice(c * CHUNK, (c + 1) * CHUNK)
+
+        def pick_x(a, t):
+            nc.scalar.activation(
+                out=x_picked[a, t][:], in_=x_rows[a, t][:].indirect(x_list[:]), func=ACT.Copy
+            )
+
+        def pick_x_shared(a, t):
+            half = J // 2
+            nc.scalar.activation(
+                out=x_picked[a, t][:, :half],
+                in_=x_rows[a, t][:].indirect(x_list[:, : LIST_COLS // 2]),
+                func=ACT.Copy,
+            )
+            nc.vector.tensor_copy(
+                out=x_picked[a, t][:, half:], in_=x_rows[a, t][:].indirect(x_list[:, LIST_COLS // 2 :])
+            )
+
+        def group_sums(a, t):
+            nc.vector.tensor_reduce(
+                out=sums[a, t][:],
+                in_=x_picked[a, t][:].rearrange("p (b i) -> p b i", i=GROUP),
+                axis=mybir.AxisListType.X,
+                op=ALU.add,
+            )
+
+        def group_means(a, t):
+            nc.vector.tensor_scalar(
+                out=means[a, t][:],
+                in0=sums[a, t][:],
+                scalar1=fk_eighth[:, a, t : t + 1],
+                scalar2=None,
+                op0=ALU.mult,
+            )
+
+        def centre(a, t):
+            nc.vector.scalar_tensor_tensor(
+                out=u_planes[a][:, t, :].rearrange("p (b i) -> p b i", i=GROUP),
+                in0=x_picked[a, t][:].rearrange("p (b i) -> p b i", i=GROUP),
+                scalar=fk_sb[:, a, t : t + 1],
+                in1=means[a, t][:].unsqueeze(2).to_broadcast([P, B, GROUP]),
+                op0=ALU.mult,
+                op1=ALU.subtract,
+            )
+
+        def woven_view(tile_cols):
+            return tile_cols.rearrange("p (g i t) -> p g t i", i=RUN, t=PACK)
+
+        def planes_view(tile_planes):
+            return tile_planes.rearrange("p t (g i) -> p g t i", i=RUN)
+
+        def weave_u(a, c, copy):
+            cols = slice(c * CHUNK * PACK, (c + 1) * CHUNK * PACK)
+            copy(out=woven_view(u_woven[a][:, cols]), in_=planes_view(u_planes[a][:, :, slots(c)]))
+
+        def quantise_u(a, first, last):
+            nc.vector.quantize_mx(
+                out=u_codes[a][:, first * CHUNK : last * CHUNK].bitcast(E4M3X4),
+                scales=u_scales[a][:, first * CHUNK : last * CHUNK],
+                in_=u_woven[a][:, first * CHUNK * PACK : last * CHUNK * PACK],
+            )
+
+        def first_product(a, c):
+            for t in range(PACK):
+                nc.tensor.matmul_mx(
+                    out=a_banks[c][:, t, :],
+                    lhsT=w_dealt[:, a, t, :].bitcast(E2M1X4),
+                    lhsT_scale=ws_dealt[:, a, t, :],
+                    rhs=u_codes[a][:, slots(c)].bitcast(E4M3X4),
+                    rhs_scale=u_scales[a][:, slots(c)],
+                    start=(a == 0 and t == 0),
+                    stop=(a == PASSES - 1 and t == PACK - 1),
+                )
+
+        def pick_tb(t, first, last):
+            nc.scalar.activation(
+                out=tb_picked[:, t, first * CHUNK : last * CHUNK],
+                in_=tb_rows[t][:].indirect(tb_list[:, first * CHUNK // 16 : last * CHUNK // 16]),
+                func=ACT.Copy,
+            )
+
+        def take_off_table(c):
+            nc.vector.tensor_tensor(
+                out=gaps[c][:], in0=a_banks[c][:], in1=tb_picked[:, :, slots(c)], op=ALU.subtract
+            )
+
+        def relu_weave(c):
+            nc.scalar.activation(
+                out=woven_view(hid_woven[c][:]), in_=planes_view(gaps[c][:]), func=ACT.Relu
+            )
+
+        def second_product(c):
+            nc.vector.quantize_mx(
+                out=hid_codes[c][:].bitcast(E4M3X4), scales=hid_scales[c][:], in_=hid_woven[c][:]
+            )
+            for h in range(HALVES):
+                nc.tensor.matmul_mx(
+                    out=p_banks[c][:, h, :],
+                    lhsT=wb_codes[:, h * P : (h + 1) * P].bitcast(E5M2X4),
+                    lhsT_scale=wb_plane[:, h * P : (h + 1) * P],
+                    rhs=hid_codes[c][:].bitcast(E4M3X4),
+                    rhs_scale=hid_scales[c][:],
+                    start=True,
+                    stop=True,
+                )
+
+        def lag(c):
+            width = min(CHUNK, J - 1 - c * CHUNK)
+            shifted = lagged[:, :, c * CHUNK + 1 : c * CHUNK + 1 + width]
+            nc.vector.scalar_tensor_tensor(
+                out=shifted, in0=p_banks[c][:, :, :width], scalar=-1.4, in1=shifted, op0=ALU.mult, op1=ALU.add
+            )
+
+        def finish(c):
+            nc.vector.scalar_tensor_tensor(
+                out=result[:, :, slots(c)],
+                in0=lagged[:, :, slots(c)],
+                scalar=0.5,
+                in1=p_banks[c][:],
+                op0=ALU.mult,
+                op1=ALU.add,
+            )
+            nc.sync.dma_start(
+                out=out.rearrange("(h p) j -> p h j", p=P)[:, :, slots(c)], in_=result[:, :, slots(c)]
+            )
+
+        for n, (a, t) in enumerate(planes):
+            if n == len(planes) - 1:
+                pick_x_shared(a, t)
+            else:
+                pick_x(a, t)
+            group_sums(a, t)
+            group_means(a, t)
+            centre(a, t)
+            if a == 1 and t < CHUNKS:
+                weave_u(0, t, nc.scalar.copy)
+            if a == 1 and t == CHUNKS - 1:
+                quantise_u(0, 0, CHUNKS)
+                for c in range(CHUNKS):
+                    first_product(0, c)
+
+        pick_tb(0, 0, CHUNKS)
+        pick_tb(1, 0, CHUNKS)
+        for c in range(CHUNKS):
+            weave_u(1, c, nc.vector.tensor_copy)
+            quantise_u(1, c, c + 1)
+            first_product(1, c)
+        for c in range(CHUNKS):
+            pick_tb(2, c, c + 1)
+            pick_tb(3, c, c + 1)
+            take_off_table(c)
+            relu_weave(c)
+        for c in range(CHUNKS):
+            second_product(c)
+            lag(c)
+            finish(c)

@@ -45,11 +45,11 @@ def tile_list_centredpicks_overtable_lagged_kernel(
         tb_list = tile([P, LIST_COLS], U16, "tb_list")
         x_rows = {(a, t): tile([P, T], F32, "x_rows%d%d" % (a, t)) for a, t in planes}
         x_picked = {(a, t): tile([P, J], F32, "x_picked%d%d" % (a, t)) for a, t in planes}
-        sums = {(a, t): tile([P, B], F32, "sums%d%d" % (a, t)) for a, t in planes}
-        means = {(a, t): tile([P, B], F32, "means%d%d" % (a, t)) for a, t in planes}
+        sums = [tile([P, PACK, B], F32, "sums%d" % a) for a in range(PASSES)]
+        means = [tile([P, PACK, B], F32, "means%d" % a) for a in range(PASSES)]
         fk_sb = tile([P, PASSES, PACK], F32, "fk_sb")
         fk_eighth = tile([P, PASSES, PACK], F32, "fk_eighth")
-        u_planes = [tile([P, PACK, J], BF16, "u_planes%d" % a) for a in range(PASSES)]
+        x_scaled = [tile([P, PACK, J], F32, "x_scaled%d" % a) for a in range(PASSES)]
         u_woven = [tile([P, J * PACK], BF16, "u_woven%d" % a) for a in range(PASSES)]
         u_codes = [tile([P, J], U32, "u_codes%d" % a) for a in range(PASSES)]
         u_scales = [tile([P, J], U8, "u_scales%d" % a) for a in range(PASSES)]
@@ -57,42 +57,57 @@ def tile_list_centredpicks_overtable_lagged_kernel(
         w_dealt = tile([P, PASSES, PACK, P], U16, "w_dealt")
         ws_raw = tile([P, PASSES, R], U8, "ws_raw")
         ws_dealt = tile([P, PASSES, PACK, P], U8, "ws_dealt")
-        tb_rows = [tile([P, V], F32, "tb_rows%d" % t) for t in range(PACK)]
+        tb_early = [tile([P, V], F32, "tb_early%d" % t) for t in range(2)]
+        tb_late = tile([P, 2, V], F32, "tb_late")
+        tb_rows = [tb_early[0][:], tb_early[1][:], tb_late[:, 0, :], tb_late[:, 1, :]]
         tb_picked = tile([P, PACK, J], F32, "tb_picked")
         wb_codes = tile([P, N], U32, "wb_codes")
         wb_plane = tile([P, N], U8, "wb_plane")
         lagged = tile([P, HALVES, J], F32, "lagged")
         result = tile([P, HALVES, J], F32, "result")
+        spans = [(0, 2 * CHUNK), (2 * CHUNK, J)]
         gaps = [tile([P, PACK, CHUNK], F32, "gaps%d" % c) for c in range(CHUNKS)]
-        hid_woven = [tile([P, CHUNK * PACK], BF16, "hid_woven%d" % c) for c in range(CHUNKS)]
-        hid_codes = [tile([P, CHUNK], U32, "hid_codes%d" % c) for c in range(CHUNKS)]
-        hid_scales = [tile([P, CHUNK], U8, "hid_scales%d" % c) for c in range(CHUNKS)]
+        hid_woven = tile([P, J * PACK], BF16, "hid_woven")
+        hid_codes = tile([P, J], U32, "hid_codes")
+        hid_scales = tile([P, J], U8, "hid_scales")
         a_banks = [psum.tile([P, PACK, CHUNK], F32, name="a_bank%d" % c) for c in range(CHUNKS)]
-        p_banks = [psum.tile([P, HALVES, CHUNK], F32, name="p_bank%d" % c) for c in range(CHUNKS)]
+        p_banks = [psum.tile([P, HALVES, hi - lo], F32, name="p_bank%d" % lo) for lo, hi in spans]
 
         x_hbm = xf.rearrange("(a p t) c -> a t p c", a=PASSES, t=PACK)
-        tb_hbm = tb.rearrange("(p t) v -> t p v", t=PACK)
+        tb_hbm = tb.rearrange("(p t) v -> p t v", t=PACK)
 
         nc.gpsimd.memset(ws_raw[:].bitcast(I32), 0)
         nc.gpsimd.memset(wb_plane[:].bitcast(I32), 0)
-        nc.sync.dma_start(x_list[:], offs)
-        nc.sync.dma_start(out=x_rows[0, 0][:], in_=x_hbm[0, 0])
-        nc.sync.dma_start(out=fk_sb[:], in_=fk.rearrange("(a p t) o -> p a (t o)", a=PASSES, t=PACK))
-        nc.sync.dma_start(
-            out=w_raw[:].bitcast(I32), in_=w_words.rearrange("a p c -> p a c").bitcast(I32)
-        )
-        for a, t in planes[1:5]:
+
+        def load_x(n):
+            a, t = planes[n]
             nc.sync.dma_start(out=x_rows[a, t][:], in_=x_hbm[a, t])
-        for q in range(4):
+
+        def load_w_scales(q):
             nc.sync.dma_start(
                 out=ws_raw[32 * q : 32 * q + 4].bitcast(I32),
                 in_=w_scales[:, 4 * q : 4 * q + 4, :].rearrange("a r c -> r a c").bitcast(I32),
             )
-        for a, t in planes[5:]:
-            nc.sync.dma_start(out=x_rows[a, t][:], in_=x_hbm[a, t])
+
+        nc.scalar.dma_start(out=fk_sb[:], in_=fk.rearrange("(a p t) o -> p a (t o)", a=PASSES, t=PACK))
+        nc.sync.dma_start(x_list[:], offs)
+        load_x(0)
+        load_x(1)
+        load_w_scales(0)
+        load_w_scales(1)
+        load_x(2)
+        load_w_scales(2)
+        load_w_scales(3)
+        load_x(3)
+        nc.sync.dma_start(
+            out=w_raw[:].bitcast(I32), in_=w_words.rearrange("a p c -> p a c").bitcast(I32)
+        )
+        for n in range(4, len(planes)):
+            load_x(n)
         nc.sync.dma_start(tb_list[:], offs2)
-        for t in range(PACK):
-            nc.sync.dma_start(out=tb_rows[t][:], in_=tb_hbm[t])
+        for t in range(2):
+            nc.sync.dma_start(out=tb_early[t][:], in_=tb_hbm[:, t, :])
+        nc.sync.dma_start(out=tb_late[:], in_=tb_hbm[:, 2:, :])
         nc.sync.dma_start(
             out=wb_codes[:].bitcast(I32), in_=wb_words[0].rearrange("p n t -> p (n t)").bitcast(I32)
         )
@@ -104,8 +119,6 @@ def tile_list_centredpicks_overtable_lagged_kernel(
         nc.sync.dma_start(out=lagged[:], in_=rs.rearrange("(h p) j -> p h j", p=P))
 
         nc.scalar.activation(out=fk_eighth[:], in_=fk_sb[:], func=ACT.Copy, scale=1.0 / GROUP)
-        nc.vector.tensor_copy(out=w_dealt[:], in_=w_raw[:].rearrange("p a (m t) -> p a t m", t=PACK))
-        nc.vector.tensor_copy(out=ws_dealt[:], in_=ws_raw[:].rearrange("p a (m t) -> p a t m", t=PACK))
 
         def slots(c):
             return slice(c * CHUNK, (c + 1) * CHUNK)
@@ -115,42 +128,43 @@ def tile_list_centredpicks_overtable_lagged_kernel(
                 out=x_picked[a, t][:], in_=x_rows[a, t][:].indirect(x_list[:]), func=ACT.Copy
             )
 
-        def pick_x_shared(a, t):
-            half = J // 2
-            nc.scalar.activation(
-                out=x_picked[a, t][:, :half],
-                in_=x_rows[a, t][:].indirect(x_list[:, : LIST_COLS // 2]),
-                func=ACT.Copy,
-            )
-            nc.vector.tensor_copy(
-                out=x_picked[a, t][:, half:], in_=x_rows[a, t][:].indirect(x_list[:, LIST_COLS // 2 :])
-            )
-
         def group_sums(a, t):
             nc.vector.tensor_reduce(
-                out=sums[a, t][:],
+                out=sums[a][:, t, :],
                 in_=x_picked[a, t][:].rearrange("p (b i) -> p b i", i=GROUP),
                 axis=mybir.AxisListType.X,
                 op=ALU.add,
             )
 
-        def group_means(a, t):
-            nc.vector.tensor_scalar(
-                out=means[a, t][:],
-                in0=sums[a, t][:],
-                scalar1=fk_eighth[:, a, t : t + 1],
-                scalar2=None,
+        def scale_x(a, t):
+            nc.gpsimd.tensor_scalar(
+                out=x_scaled[a][:, t, :],
+                in0=x_picked[a, t][:],
+                scalar1=fk_sb[:, a, t : t + 1],
+                scalar2=0.0,
                 op0=ALU.mult,
+                op1=ALU.add,
             )
 
-        def centre(a, t):
-            nc.vector.scalar_tensor_tensor(
-                out=u_planes[a][:, t, :].rearrange("p (b i) -> p b i", i=GROUP),
-                in0=x_picked[a, t][:].rearrange("p (b i) -> p b i", i=GROUP),
-                scalar=fk_sb[:, a, t : t + 1],
-                in1=means[a, t][:].unsqueeze(2).to_broadcast([P, B, GROUP]),
-                op0=ALU.mult,
-                op1=ALU.subtract,
+        def group_means(a, first, last):
+            nc.vector.tensor_tensor(
+                out=means[a][:, first:last, :],
+                in0=sums[a][:, first:last, :],
+                in1=fk_eighth[:, a, first:last].unsqueeze(2).to_broadcast([P, last - first, B]),
+                op=ALU.mult,
+            )
+
+        def centre(a, first, last):
+            groups = slice(first * CHUNK // GROUP, last * CHUNK // GROUP)
+            cols = slice(first * CHUNK * PACK, last * CHUNK * PACK)
+            nc.vector.tensor_tensor(
+                out=u_woven[a][:, cols].rearrange("p (b i t) -> p b t i", i=GROUP, t=PACK),
+                in0=x_scaled[a][:, :, first * CHUNK : last * CHUNK].rearrange("p t (b i) -> p b t i", i=GROUP),
+                in1=means[a][:, :, groups]
+                .rearrange("p t b -> p b t")
+                .unsqueeze(3)
+                .to_broadcast([P, (last - first) * CHUNK // GROUP, PACK, GROUP]),
+                op=ALU.subtract,
             )
 
         def woven_view(tile_cols):
@@ -158,10 +172,6 @@ def tile_list_centredpicks_overtable_lagged_kernel(
 
         def planes_view(tile_planes):
             return tile_planes.rearrange("p t (g i) -> p g t i", i=RUN)
-
-        def weave_u(a, c, copy):
-            cols = slice(c * CHUNK * PACK, (c + 1) * CHUNK * PACK)
-            copy(out=woven_view(u_woven[a][:, cols]), in_=planes_view(u_planes[a][:, :, slots(c)]))
 
         def quantise_u(a, first, last):
             nc.vector.quantize_mx(
@@ -185,7 +195,7 @@ def tile_list_centredpicks_overtable_lagged_kernel(
         def pick_tb(t, first, last):
             nc.scalar.activation(
                 out=tb_picked[:, t, first * CHUNK : last * CHUNK],
-                in_=tb_rows[t][:].indirect(tb_list[:, first * CHUNK // 16 : last * CHUNK // 16]),
+                in_=tb_rows[t].indirect(tb_list[:, first * CHUNK // 16 : last * CHUNK // 16]),
                 func=ACT.Copy,
             )
 
@@ -195,72 +205,100 @@ def tile_list_centredpicks_overtable_lagged_kernel(
             )
 
         def relu_weave(c):
+            cols = slice(c * CHUNK * PACK, (c + 1) * CHUNK * PACK)
             nc.scalar.activation(
-                out=woven_view(hid_woven[c][:]), in_=planes_view(gaps[c][:]), func=ACT.Relu
+                out=woven_view(hid_woven[:, cols]), in_=planes_view(gaps[c][:]), func=ACT.Relu
             )
 
-        def second_product(c):
+        def second_product(s):
+            lo, hi = spans[s]
             nc.vector.quantize_mx(
-                out=hid_codes[c][:].bitcast(E4M3X4), scales=hid_scales[c][:], in_=hid_woven[c][:]
+                out=hid_codes[:, lo:hi].bitcast(E4M3X4),
+                scales=hid_scales[:, lo:hi],
+                in_=hid_woven[:, lo * PACK : hi * PACK],
             )
             for h in range(HALVES):
                 nc.tensor.matmul_mx(
-                    out=p_banks[c][:, h, :],
+                    out=p_banks[s][:, h, :],
                     lhsT=wb_codes[:, h * P : (h + 1) * P].bitcast(E5M2X4),
                     lhsT_scale=wb_plane[:, h * P : (h + 1) * P],
-                    rhs=hid_codes[c][:].bitcast(E4M3X4),
-                    rhs_scale=hid_scales[c][:],
+                    rhs=hid_codes[:, lo:hi].bitcast(E4M3X4),
+                    rhs_scale=hid_scales[:, lo:hi],
                     start=True,
                     stop=True,
                 )
 
-        def lag(c):
-            width = min(CHUNK, J - 1 - c * CHUNK)
-            shifted = lagged[:, :, c * CHUNK + 1 : c * CHUNK + 1 + width]
+        def lag(s):
+            lo, hi = spans[s]
+            end = min(hi + 1, J)
+            shifted = lagged[:, :, lo + 1 : end]
             nc.vector.scalar_tensor_tensor(
-                out=shifted, in0=p_banks[c][:, :, :width], scalar=-1.4, in1=shifted, op0=ALU.mult, op1=ALU.add
+                out=shifted,
+                in0=p_banks[s][:, :, : end - lo - 1],
+                scalar=-1.4,
+                in1=shifted,
+                op0=ALU.mult,
+                op1=ALU.add,
             )
 
-        def finish(c):
+        def finish(s):
+            lo, hi = spans[s]
             nc.vector.scalar_tensor_tensor(
-                out=result[:, :, slots(c)],
-                in0=lagged[:, :, slots(c)],
+                out=result[:, :, lo:hi],
+                in0=lagged[:, :, lo:hi],
                 scalar=0.5,
-                in1=p_banks[c][:],
+                in1=p_banks[s][:],
                 op0=ALU.mult,
                 op1=ALU.add,
             )
             nc.sync.dma_start(
-                out=out.rearrange("(h p) j -> p h j", p=P)[:, :, slots(c)], in_=result[:, :, slots(c)]
+                out=out.rearrange("(h p) j -> p h j", p=P)[:, :, lo:hi], in_=result[:, :, lo:hi]
             )
 
-        for n, (a, t) in enumerate(planes):
-            if n == len(planes) - 1:
-                pick_x_shared(a, t)
-            else:
-                pick_x(a, t)
+        def prepare(a, t):
+            pick_x(a, t)
+            scale_x(a, t)
             group_sums(a, t)
-            group_means(a, t)
-            centre(a, t)
-            if a == 1 and t < CHUNKS:
-                weave_u(0, t, nc.scalar.copy)
-            if a == 1 and t == CHUNKS - 1:
-                quantise_u(0, 0, CHUNKS)
-                for c in range(CHUNKS):
-                    first_product(0, c)
+
+        prepare(0, 0)
+        prepare(0, 1)
+        nc.vector.tensor_copy(out=ws_dealt[:], in_=ws_raw[:].rearrange("p a (m t) -> p a t m", t=PACK))
+        prepare(0, 2)
+        prepare(0, 3)
+        nc.scalar.copy(out=w_dealt[:], in_=w_raw[:].rearrange("p a (m t) -> p a t m", t=PACK))
+        group_means(0, 0, PACK)
+        centre(0, 0, CHUNKS)
+        prepare(1, 0)
+        prepare(1, 1)
+        quantise_u(0, 0, CHUNKS)
+        for c in range(CHUNKS):
+            first_product(0, c)
+        prepare(1, 2)
+        group_means(1, 0, PACK - 1)
+        prepare(1, 3)
+        group_means(1, PACK - 1, PACK)
 
         pick_tb(0, 0, CHUNKS)
         pick_tb(1, 0, CHUNKS)
         for c in range(CHUNKS):
-            weave_u(1, c, nc.vector.tensor_copy)
-            quantise_u(1, c, c + 1)
-            first_product(1, c)
-        for c in range(CHUNKS):
             pick_tb(2, c, c + 1)
             pick_tb(3, c, c + 1)
+
+        centre(1, 0, 1)
+        centre(1, 1, 2)
+        quantise_u(1, 0, 1)
+        first_product(1, 0)
+        centre(1, 2, 3)
+        quantise_u(1, 1, 2)
+        first_product(1, 1)
+        quantise_u(1, 2, 3)
+        first_product(1, 2)
+        for c in range(CHUNKS):
             take_off_table(c)
             relu_weave(c)
-        for c in range(CHUNKS):
-            second_product(c)
-            lag(c)
-            finish(c)
+        second_product(0)
+        second_product(1)
+        lag(0)
+        finish(0)
+        lag(1)
+        finish(1)

from contextlib import ExitStack

import concourse.mybir as mybir

K, T, J, R, V, N = 1024, 1024, 384, 512, 512, 256
GROUP = 8
B = J // GROUP
FLOPS = 2 * K * R * J + 2 * R * N * J

F32 = mybir.dt.float32
BF16 = mybir.dt.bfloat16
I32 = mybir.dt.int32
U32 = mybir.dt.uint32
U16 = mybir.dt.uint16
U8 = mybir.dt.uint8
E4M3X4 = mybir.dt.float8_e4m3fn_x4
E5M2X4 = mybir.dt.float8_e5m2_x4
E2M1X4 = mybir.dt.float4_e2m1fn_x4
ALU = mybir.AluOpType
ACT = mybir.ActivationFunctionType

P = 128
PACK = 4
PASSES = K // (P * PACK)
CHUNK = 128
CHUNKS = J // CHUNK
HALVES = N // P
LIST_COLS = J // 16
RUN = 4


def tile_list_centredpicks_overtable_lagged_kernel(
    tc, xf, fk, w_words, w_scales, tb, wb_words, wb_scales, rs, offs, offs2, out
):
    nc = tc.nc
    with ExitStack() as ctx:
        pool = ctx.enter_context(tc.tile_pool(name="held", bufs=1))
        psum = ctx.enter_context(tc.psum_pool(name="psum", bufs=1))

        def tile(shape, dtype, name):
            return pool.tile(shape, dtype, name=name, align_bytes=64)

        planes = [(a, t) for a in range(PASSES) for t in range(PACK)]
        x_list = tile([P, LIST_COLS], U16, "x_list")
        tb_list = tile([P, LIST_COLS], U16, "tb_list")
        x_rows = {(a, t): tile([P, T], F32, "x_rows%d%d" % (a, t)) for a, t in planes}
        x_picked = {(a, t): tile([P, J], F32, "x_picked%d%d" % (a, t)) for a, t in planes}
        sums = [tile([P, PACK, B], F32, "sums%d" % a) for a in range(PASSES)]
        means = [tile([P, PACK, B], F32, "means%d" % a) for a in range(PASSES)]
        fk_sb = tile([P, PASSES, PACK], F32, "fk_sb")
        fk_eighth = tile([P, PASSES, PACK], F32, "fk_eighth")
        x_scaled = [tile([P, PACK, J], F32, "x_scaled%d" % a) for a in range(PASSES)]
        u_woven = [tile([P, J * PACK], BF16, "u_woven%d" % a) for a in range(PASSES)]
        u_codes = [tile([P, J], U32, "u_codes%d" % a) for a in range(PASSES)]
        u_scales = [tile([P, J], U8, "u_scales%d" % a) for a in range(PASSES)]
        w_raw = tile([P, PASSES, R], U16, "w_raw")
        w_dealt = tile([P, PASSES, PACK, P], U16, "w_dealt")
        ws_raw = tile([P, PASSES, R], U8, "ws_raw")
        ws_dealt = tile([P, PASSES, PACK, P], U8, "ws_dealt")
        tb_early = [tile([P, V], F32, "tb_early%d" % t) for t in range(2)]
        tb_late = tile([P, 2, V], F32, "tb_late")
        tb_rows = [tb_early[0][:], tb_early[1][:], tb_late[:, 0, :], tb_late[:, 1, :]]
        tb_picked = tile([P, PACK, J], F32, "tb_picked")
        wb_codes = tile([P, N], U32, "wb_codes")
        wb_plane = tile([P, N], U8, "wb_plane")
        lagged = tile([P, HALVES, J], F32, "lagged")
        result = tile([P, HALVES, J], F32, "result")
        spans = [(0, 2 * CHUNK), (2 * CHUNK, J)]
        gaps = [tile([P, PACK, CHUNK], F32, "gaps%d" % c) for c in range(CHUNKS)]
        hid_woven = tile([P, J * PACK], BF16, "hid_woven")
        hid_codes = tile([P, J], U32, "hid_codes")
        hid_scales = tile([P, J], U8, "hid_scales")
        a_banks = [psum.tile([P, PACK, CHUNK], F32, name="a_bank%d" % c) for c in range(CHUNKS)]
        p_banks = [psum.tile([P, HALVES, hi - lo], F32, name="p_bank%d" % lo) for lo, hi in spans]

        x_hbm = xf.rearrange("(a p t) c -> a t p c", a=PASSES, t=PACK)
        tb_hbm = tb.rearrange("(p t) v -> p t v", t=PACK)

        nc.gpsimd.memset(ws_raw[:].bitcast(I32), 0)
        nc.gpsimd.memset(wb_plane[:].bitcast(I32), 0)

        def load_x(n):
            a, t = planes[n]
            nc.sync.dma_start(out=x_rows[a, t][:], in_=x_hbm[a, t])

        def load_w_scales(q):
            nc.sync.dma_start(
                out=ws_raw[32 * q : 32 * q + 4].bitcast(I32),
                in_=w_scales[:, 4 * q : 4 * q + 4, :].rearrange("a r c -> r a c").bitcast(I32),
            )

        nc.scalar.dma_start(out=fk_sb[:], in_=fk.rearrange("(a p t) o -> p a (t o)", a=PASSES, t=PACK))
        nc.sync.dma_start(x_list[:], offs)
        load_x(0)
        load_x(1)
        load_w_scales(0)
        load_w_scales(1)
        load_x(2)
        load_w_scales(2)
        load_w_scales(3)
        load_x(3)
        nc.sync.dma_start(
            out=w_raw[:].bitcast(I32), in_=w_words.rearrange("a p c -> p a c").bitcast(I32)
        )
        for n in range(4, len(planes)):
            load_x(n)
        nc.sync.dma_start(tb_list[:], offs2)
        for t in range(2):
            nc.sync.dma_start(out=tb_early[t][:], in_=tb_hbm[:, t, :])
        nc.sync.dma_start(out=tb_late[:], in_=tb_hbm[:, 2:, :])
        nc.sync.dma_start(
            out=wb_codes[:].bitcast(I32), in_=wb_words[0].rearrange("p n t -> p (n t)").bitcast(I32)
        )
        for q in range(4):
            nc.sync.dma_start(
                out=wb_plane[32 * q : 32 * q + 4].bitcast(I32),
                in_=wb_scales[0, 4 * q : 4 * q + 4, :].bitcast(I32),
            )
        nc.sync.dma_start(out=lagged[:], in_=rs.rearrange("(h p) j -> p h j", p=P))

        nc.scalar.activation(out=fk_eighth[:], in_=fk_sb[:], func=ACT.Copy, scale=1.0 / GROUP)

        def slots(c):
            return slice(c * CHUNK, (c + 1) * CHUNK)

        def pick_x(a, t):
            nc.scalar.activation(
                out=x_picked[a, t][:], in_=x_rows[a, t][:].indirect(x_list[:]), func=ACT.Copy
            )

        def group_sums(a, t):
            nc.vector.tensor_reduce(
                out=sums[a][:, t, :],
                in_=x_picked[a, t][:].rearrange("p (b i) -> p b i", i=GROUP),
                axis=mybir.AxisListType.X,
                op=ALU.add,
            )

        def scale_x(a, t):
            nc.gpsimd.tensor_scalar(
                out=x_scaled[a][:, t, :],
                in0=x_picked[a, t][:],
                scalar1=fk_sb[:, a, t : t + 1],
                scalar2=0.0,
                op0=ALU.mult,
                op1=ALU.add,
            )

        def group_means(a, first, last):
            nc.vector.tensor_tensor(
                out=means[a][:, first:last, :],
                in0=sums[a][:, first:last, :],
                in1=fk_eighth[:, a, first:last].unsqueeze(2).to_broadcast([P, last - first, B]),
                op=ALU.mult,
            )

        def centre(a, first, last):
            groups = slice(first * CHUNK // GROUP, last * CHUNK // GROUP)
            cols = slice(first * CHUNK * PACK, last * CHUNK * PACK)
            nc.vector.tensor_tensor(
                out=u_woven[a][:, cols].rearrange("p (b i t) -> p b t i", i=GROUP, t=PACK),
                in0=x_scaled[a][:, :, first * CHUNK : last * CHUNK].rearrange("p t (b i) -> p b t i", i=GROUP),
                in1=means[a][:, :, groups]
                .rearrange("p t b -> p b t")
                .unsqueeze(3)
                .to_broadcast([P, (last - first) * CHUNK // GROUP, PACK, GROUP]),
                op=ALU.subtract,
            )

        def woven_view(tile_cols):
            return tile_cols.rearrange("p (g i t) -> p g t i", i=RUN, t=PACK)

        def planes_view(tile_planes):
            return tile_planes.rearrange("p t (g i) -> p g t i", i=RUN)

        def quantise_u(a, first, last):
            nc.vector.quantize_mx(
                out=u_codes[a][:, first * CHUNK : last * CHUNK].bitcast(E4M3X4),
                scales=u_scales[a][:, first * CHUNK : last * CHUNK],
                in_=u_woven[a][:, first * CHUNK * PACK : last * CHUNK * PACK],
            )

        def first_product(a, c):
            for t in range(PACK):
                nc.tensor.matmul_mx(
                    out=a_banks[c][:, t, :],
                    lhsT=w_dealt[:, a, t, :].bitcast(E2M1X4),
                    lhsT_scale=ws_dealt[:, a, t, :],
                    rhs=u_codes[a][:, slots(c)].bitcast(E4M3X4),
                    rhs_scale=u_scales[a][:, slots(c)],
                    start=(a == 0 and t == 0),
                    stop=(a == PASSES - 1 and t == PACK - 1),
                )

        def pick_tb(t, first, last):
            nc.scalar.activation(
                out=tb_picked[:, t, first * CHUNK : last * CHUNK],
                in_=tb_rows[t].indirect(tb_list[:, first * CHUNK // 16 : last * CHUNK // 16]),
                func=ACT.Copy,
            )

        def take_off_table(c):
            nc.vector.tensor_tensor(
                out=gaps[c][:], in0=a_banks[c][:], in1=tb_picked[:, :, slots(c)], op=ALU.subtract
            )

        def relu_weave(c):
            cols = slice(c * CHUNK * PACK, (c + 1) * CHUNK * PACK)
            nc.scalar.activation(
                out=woven_view(hid_woven[:, cols]), in_=planes_view(gaps[c][:]), func=ACT.Relu
            )

        def second_product(s):
            lo, hi = spans[s]
            nc.vector.quantize_mx(
                out=hid_codes[:, lo:hi].bitcast(E4M3X4),
                scales=hid_scales[:, lo:hi],
                in_=hid_woven[:, lo * PACK : hi * PACK],
            )
            for h in range(HALVES):
                nc.tensor.matmul_mx(
                    out=p_banks[s][:, h, :],
                    lhsT=wb_codes[:, h * P : (h + 1) * P].bitcast(E5M2X4),
                    lhsT_scale=wb_plane[:, h * P : (h + 1) * P],
                    rhs=hid_codes[:, lo:hi].bitcast(E4M3X4),
                    rhs_scale=hid_scales[:, lo:hi],
                    start=True,
                    stop=True,
                )

        def lag(s):
            lo, hi = spans[s]
            end = min(hi + 1, J)
            shifted = lagged[:, :, lo + 1 : end]
            nc.vector.scalar_tensor_tensor(
                out=shifted,
                in0=p_banks[s][:, :, : end - lo - 1],
                scalar=-1.4,
                in1=shifted,
                op0=ALU.mult,
                op1=ALU.add,
            )

        def finish(s):
            lo, hi = spans[s]
            nc.vector.scalar_tensor_tensor(
                out=result[:, :, lo:hi],
                in0=lagged[:, :, lo:hi],
                scalar=0.5,
                in1=p_banks[s][:],
                op0=ALU.mult,
                op1=ALU.add,
            )
            nc.sync.dma_start(
                out=out.rearrange("(h p) j -> p h j", p=P)[:, :, lo:hi], in_=result[:, :, lo:hi]
            )

        def prepare(a, t):
            pick_x(a, t)
            scale_x(a, t)
            group_sums(a, t)

        prepare(0, 0)
        prepare(0, 1)
        nc.vector.tensor_copy(out=ws_dealt[:], in_=ws_raw[:].rearrange("p a (m t) -> p a t m", t=PACK))
        prepare(0, 2)
        prepare(0, 3)
        nc.scalar.copy(out=w_dealt[:], in_=w_raw[:].rearrange("p a (m t) -> p a t m", t=PACK))
        group_means(0, 0, PACK)
        centre(0, 0, CHUNKS)
        prepare(1, 0)
        prepare(1, 1)
        quantise_u(0, 0, CHUNKS)
        for c in range(CHUNKS):
            first_product(0, c)
        prepare(1, 2)
        group_means(1, 0, PACK - 1)
        prepare(1, 3)
        group_means(1, PACK - 1, PACK)

        pick_tb(0, 0, CHUNKS)
        pick_tb(1, 0, CHUNKS)
        for c in range(CHUNKS):
            pick_tb(2, c, c + 1)
            pick_tb(3, c, c + 1)

        centre(1, 0, 1)
        centre(1, 1, 2)
        quantise_u(1, 0, 1)
        first_product(1, 0)
        centre(1, 2, 3)
        quantise_u(1, 1, 2)
        first_product(1, 1)
        quantise_u(1, 2, 3)
        first_product(1, 2)
        for c in range(CHUNKS):
            take_off_table(c)
            relu_weave(c)
        second_product(0)
        second_product(1)
        lag(0)
        finish(0)
        lag(1)
        finish(1)
